import numpy as np
import ml_dtypes


def mxq(x, axis, fmt="e4m3"):
    dtype, down = {"e4m3": (ml_dtypes.float8_e4m3fn, 7), "e5m2": (ml_dtypes.float8_e5m2, 14)}[fmt]
    v = np.moveaxis(np.asarray(x, np.float32).astype(ml_dtypes.bfloat16).astype(np.float64), axis, -1)
    blocks = v.reshape(v.shape[:-1] + (-1, 32))
    amax = np.abs(blocks).max(-1, keepdims=True)
    byte = np.maximum(np.where(amax > 0, np.frexp(amax)[1] - 1 + 127, 0) - down, 1)
    scale = np.exp2(byte - 127.0)
    codes = (blocks / scale).astype(np.float32).astype(dtype).astype(np.float64)
    return np.moveaxis((codes * scale).reshape(v.shape), -1, axis)


WIDE = False


def mx_kscale(k):
    if not WIDE:
        return np.ones(k)
    levels = np.array([10, -10, 5, -5, 0])
    if k % 512:
        return np.exp2(np.random.permutation(np.resize(levels, k // 32))).repeat(32)
    a = np.empty((k // 512, 16))
    for p in range(k // 512):
        a[p, :8] = np.random.permutation(np.resize(levels, 8))
        for g in range(8):
            far = levels[np.abs(levels - a[p, g]) >= 10]
            a[p, g + 8] = far[np.random.randint(len(far))]
    return np.exp2(a.ravel()).repeat(32)


def f64(x):
    return np.asarray(x).astype(np.float64)


def striped(idx):
    return np.tile(idx.reshape(-1, 16).T, (8, 1)).astype(np.uint16)


def unstriped(offs):
    return offs[:16].T.reshape(-1).astype(np.int64)


E2M1 = np.array([0.0, 0.5, 1.0, 1.5, 2.0, 3.0, 4.0, 6.0, -0.0, -0.5, -1.0, -1.5, -2.0, -3.0, -4.0, -6.0])


def pack_weight(w, fmt):
    k, n = w.shape
    w = f64(np.asarray(w, np.float32).astype(ml_dtypes.bfloat16)).reshape(k // 32, 32, n)
    amax = np.abs(w).max(1)
    if fmt == "e4m3":
        byte = np.frexp(amax)[1] - 1 + 127 - 7
    else:
        mant, ex = np.frexp(amax / 6.0)
        byte = np.where(mant > 0.5, ex, ex - 1) + 127
    byte = np.clip(np.where(amax > 0, byte, 1), 1, 254)
    scaled = (w * np.exp2(127.0 - byte)[:, None, :]).reshape(k, n).astype(np.float32)
    by_word = np.ascontiguousarray(scaled.reshape(k // 512, 128, 4, n).transpose(0, 1, 3, 2))
    if fmt == "e4m3":
        words = by_word.astype(ml_dtypes.float8_e4m3fn).view(np.uint8)
    else:
        c = by_word.astype(ml_dtypes.float4_e2m1fn).view(np.uint8) & 0xF
        words = (c[..., 0::2] | (c[..., 1::2] << 4)).reshape(k // 512, 128, 2 * n)
    return np.ascontiguousarray(words), np.ascontiguousarray(byte.astype(np.uint8).reshape(k // 512, 16, n))


def unpack_weight(words, scales, fmt):
    g, _, n = scales.shape
    words = np.ascontiguousarray(words).reshape(g, 128, n, -1)
    if fmt == "e4m3":
        vals = words.view(ml_dtypes.float8_e4m3fn).astype(np.float64)
    else:
        nib = np.empty((g, 128, n, 4), np.uint8)
        nib[..., 0::2] = words & 0xF
        nib[..., 1::2] = words >> 4
        vals = E2M1[nib]
    vals = vals * np.repeat(np.exp2(scales.astype(np.float64) - 127.0), 8, axis=1)[..., None]
    return vals.transpose(0, 1, 3, 2).reshape(g * 512, n)


def gelu(v):
    return 0.5 * v * (1.0 + np.tanh(np.sqrt(2.0 / np.pi) * (v + 0.044715 * v**3)))


def twice(P):
    return np.random.permutation(np.repeat(np.arange(P), 2))


def bf(x):
    return np.asarray(x, np.float32).astype(ml_dtypes.bfloat16)


def planes(Y):
    n, m = Y.shape
    b = f64(bf(Y)).reshape(n // 32, 32, m)
    amax = np.abs(b).max(1)
    byte = np.clip(np.where(amax > 0, np.frexp(amax)[1] - 1 + 127 - 7, 1), 1, 254)
    codes = (b * np.exp2(127.0 - byte)[:, None, :]).reshape(n, m).astype(np.float32).astype(ml_dtypes.float8_e4m3fn).view(np.uint8)
    words = codes.reshape(n // 512, 128, 4, m).transpose(0, 1, 3, 2)
    return np.ascontiguousarray(words), np.ascontiguousarray(byte.astype(np.uint8).reshape(n // 512, 16, m))


K, T, H, S, P = 1024, 2048, 1024, 1024, 512


def setup_inputs():
    n = np.random.standard_normal
    s = mx_kscale(K)[:, None]
    u = mx_kscale(H)[:, None]
    size = np.exp(0.8 * n(H))
    d = {}
    d["tab_words"], d["tab_scales"] = pack_weight(n((K, T)) * s, "e4m3")
    d["offs"] = striped(np.random.permutation(T)[:S])
    d["pos1"] = striped(np.random.permutation(S)[:P])
    d["pos2"] = striped(np.random.permutation(S)[:P])
    d["pos3"] = striped(twice(P))
    d["w1"] = (n((K, H)) / s * u.T / K ** 0.5).astype(np.float32)
    d["b1"] = (0.5 * n(H) * u[:, 0]).astype(np.float32)
    d["w4_words"], d["w4_scales"] = pack_weight(1.5 * n((H, H)) / u / H ** 0.5, "e2m1")
    d["b2"] = (0.6 * n(H)).astype(np.float32)
    d["amp"] = size.astype(np.float32)
    d["w3"] = (0.8 * n((H, H)) / u * size[None, :] / H ** 0.5).astype(np.float32)
    d["gh"] = (0.7 * np.exp(0.3 * n(H)) * size / u[:, 0]).astype(np.float32)
    return d


def reference(tab_words, tab_scales, offs, pos1, pos2, pos3, w1, b1, w4_words, w4_scales, b2, amp, w3, gh):
    v = unpack_weight(tab_words, tab_scales, "e4m3")[:, unstriped(offs)]
    h = (mxq(f64(w1), 0, "e4m3").T @ v) + f64(b1)[:, None]
    x1 = mxq(h[:, unstriped(pos1)], 0, "e4m3")
    x2 = mxq(h[:, unstriped(pos2)], 0, "e4m3")
    w4 = unpack_weight(w4_words, w4_scales, "e2m1")
    bent = np.tanh((w4.T @ x1) + f64(b2)[:, None])
    straight = mxq(f64(w3), 0, "e4m3").T @ x2
    cut = f64(amp)[:, None] * bent + straight
    y = cut[:, unstriped(pos3)] - f64(gh)[:, None] * h
    words, scales = planes(y)
    return y, words, scales

@@ -1,0 +1,297 @@
+from contextlib import ExitStack
+
+import concourse.mybir as mybir
+
+K, T, H, S, CUTS = 1024, 2048, 1024, 1024, 512
+FLOPS = 2 * K * H * S + 2 * 2 * H * H * CUTS
+
+F32 = mybir.dt.float32
+BF16 = mybir.dt.bfloat16
+I32 = mybir.dt.int32
+U32 = mybir.dt.uint32
+U16 = mybir.dt.uint16
+U8 = mybir.dt.uint8
+FP8X4 = mybir.dt.float8_e4m3fn_x4
+FP4X4 = mybir.dt.float4_e2m1fn_x4
+ACT = mybir.ActivationFunctionType
+ALU = mybir.AluOpType
+
+P = 128
+PACK = 4
+GROUP = P * PACK
+GROUPS = 2
+BANK = 512
+SLICES = ((0, 384), (384, 768), (768, 1024))
+Y_SLOTS = (0, 1, 9, 0, 1, 9)
+FUSED = True
+
+
+def tile_list_slab_bookmatch_features_kernel(
+    tc, tab_words, tab_scales, offs, pos1, pos2, pos3, w1, b1, w4_words, w4_scales, b2, amp, w3, gh,
+    out_0, out_1, out_2,
+):
+    nc = tc.nc
+    with ExitStack() as ctx:
+        keep = ctx.enter_context(tc.tile_pool(name="keep", bufs=1))
+        big = ctx.enter_context(tc.tile_pool(name="big", bufs=1))
+        work = ctx.enter_context(tc.tile_pool(name="work", bufs=3))
+        psum = ctx.enter_context(tc.psum_pool(name="psum", bufs=1))
+
+        def load_list(src, name):
+            t = keep.tile(list(src.shape), U16, name=name)
+            nc.sync.dma_start(out=t[:], in_=src)
+            return t
+
+        def load_dealt(vec, name):
+            t = keep.tile([P, GROUPS, PACK], F32, name=name)
+            nc.sync.dma_start(out=t[:], in_=vec.rearrange("(g p t) -> p g t", g=GROUPS, t=PACK))
+            return t
+
+        def load_weight(w, g, a, slot, parts=1):
+            raw = big.tile([P, PACK, GROUP], F32, name="raw", tag="big%d" % slot)
+            rows = w[a * GROUP:(a + 1) * GROUP, g * GROUP:(g + 1) * GROUP]
+            rows = rows.rearrange("(p j) c -> p j c", j=PACK)
+            n = GROUP // parts
+            for i in range(parts):
+                nc.sync.dma_start(out=raw[:, :, i * n:(i + 1) * n], in_=rows[:, :, i * n:(i + 1) * n])
+            return raw
+
+        def load_table(a):
+            t = big.tile([P, T], I32, name="tabw", tag="big%d" % a)
+            nc.sync.dma_start(out=t[:], in_=tab_words[a].rearrange("p t i -> p (t i)").bitcast(I32))
+            return t
+
+        def copy_on(eng, out, in_):
+            if eng == "s":
+                nc.scalar.copy(out=out, in_=in_)
+            else:
+                nc.vector.tensor_copy(out=out, in_=in_)
+
+        def round_weight(raw, engines):
+            dealt = work.tile([P, GROUP * PACK], BF16, name="dealt", tag="dealt", align_bytes=64)
+            dst = dealt[:].rearrange("p (t m j) -> p m t j", t=PACK, j=PACK)
+            src = raw[:].rearrange("p j (m t) -> p m t j", t=PACK)
+            half = P // 2
+            for i, eng in enumerate(engines):
+                copy_on(eng, dst[:, i * half:(i + 1) * half], src[:, i * half:(i + 1) * half])
+            return dealt
+
+        def quantise(grouped, name):
+            codes = keep.tile([P, GROUP], U32, name=name + "c", align_bytes=64)
+            scales = keep.tile([P, GROUP], U8, name=name + "s", align_bytes=64)
+            nc.vector.quantize_mx(out=codes[:].bitcast(FP8X4), scales=scales[:], in_=grouped[:])
+            return codes, scales
+
+        def interleave(eng, out, planes):
+            copy_on(eng, out.rearrange("p (c i t) -> p c t i", i=4, t=PACK),
+                    planes.rearrange("p t (c i) -> p c t i", i=4))
+
+        tab_s = keep.tile([P, T], U8, name="tab_s")
+        w4_s = keep.tile([P, GROUPS, H], U8, name="w4_s", align_bytes=64)
+        nc.vector.memset(tab_s[:].bitcast(I32), 0)
+        nc.gpsimd.memset(w4_s[:].bitcast(I32), 0)
+        offs_t = load_list(offs, "offs_t")
+        rows_s = keep.tile([P, T // 4], I32, name="rows_s")
+        for q in range(4):
+            nc.sync.dma_start(out=rows_s[32 * q:32 * q + 8, :], in_=tab_scales[:, 4 * q:4 * q + 4, :].bitcast(I32))
+        for q in range(4):
+            nc.vector.tensor_copy(out=tab_s[32 * q:32 * q + 8, :].bitcast(I32), in_=rows_s[32 * q:32 * q + 8, :])
+        tab_w = [load_table(0), load_table(1)]
+        w1_raw = {}
+        w1_raw[0, 0] = load_weight(w1, 0, 0, 2)
+        w1_raw[0, 1] = load_weight(w1, 0, 1, 3, 2)
+        b1_t = load_dealt(b1, "b1_t")
+        gh_t = load_dealt(gh, "gh_t")
+        w1_raw[1, 0] = load_weight(w1, 1, 0, 4)
+        w1_raw[1, 1] = load_weight(w1, 1, 1, 5)
+        pos1_t = load_list(pos1, "pos1_t")
+        pos2_t = load_list(pos2, "pos2_t")
+        pos3_t = load_list(pos3, "pos3_t")
+        amp_t = load_dealt(amp, "amp_t")
+        b2_t = keep.tile([P, H // P], F32, name="b2_t")
+        with nc.allow_non_contiguous_dma(reason="one bias value for each partition"):
+            nc.sync.dma_start(out=b2_t[:], in_=b2.rearrange("(c p) -> p c", p=P))
+        for q in range(4):
+            nc.sync.dma_start(out=w4_s[32 * q:32 * q + 4, :, :].bitcast(I32),
+                              in_=w4_scales[:, 4 * q:4 * q + 4, :].rearrange("a q c -> q a c").bitcast(I32))
+        w4_w = keep.tile([P, GROUPS, 2 * H], U8, name="w4_w", align_bytes=64)
+        nc.sync.dma_start(out=w4_w[:].bitcast(I32), in_=w4_words.rearrange("a p c -> p a c").bitcast(I32))
+        w3_raw = {}
+        for g in range(GROUPS):
+            for a in range(GROUPS):
+                w3_raw[g, a] = load_weight(w3, g, a, 2 * g + a)
+
+        v_s = keep.tile([P, S], U8, name="v_s", align_bytes=64)
+        nc.vector.tensor_copy(out=v_s[:], in_=tab_s[:].indirect(offs_t[:]))
+        v_w = []
+        for a in range(GROUPS):
+            t = keep.tile([P, S], U32, name="v_w%d" % a, align_bytes=64)
+            nc.vector.tensor_copy(out=t[:], in_=tab_w[a][:].bitcast(U32).indirect(offs_t[:]))
+            v_w.append(t)
+
+        neg_gh = keep.tile([P, GROUPS, PACK], F32, name="neg_gh")
+        nc.gpsimd.tensor_scalar(out=neg_gh[:], in0=gh_t[:], scalar1=-1.0, scalar2=0.0, op0=ALU.mult, op1=ALU.add)
+
+        w1_q = {}
+        h = {}
+
+        def first_stage(g):
+            for t in range(PACK):
+                h[g, t] = keep.tile([P, S], F32, name="h%d%d" % (g, t))
+                for c0 in range(0, S, BANK):
+                    acc = psum.tile([P, BANK], F32, name="h_acc", tag="bank%d" % (2 * t + c0 // BANK))
+                    for a in (1, 0):
+                        codes, scales = w1_q[g, a]
+                        nc.tensor.matmul_mx(
+                            out=acc[:],
+                            lhsT=codes[:, t * P:(t + 1) * P].bitcast(FP8X4), lhsT_scale=scales[:, t * P:(t + 1) * P],
+                            rhs=v_w[a][:, c0:c0 + BANK].bitcast(FP8X4), rhs_scale=v_s[4 * a:P, c0:c0 + BANK],
+                            start=(a == 1), stop=(a == 0))
+                    nc.scalar.activation(out=h[g, t][:, c0:c0 + BANK], in_=acc[:], func=ACT.Identity,
+                                         bias=b1_t[:, g, t:t + 1])
+
+        d00 = round_weight(w1_raw[0, 0], "ss")
+        d01 = round_weight(w1_raw[0, 1], "sv")
+        w1_q[0, 0] = quantise(d00, "w1q00")
+        w1_q[0, 1] = quantise(d01, "w1q01")
+        first_stage(0)
+        d10 = round_weight(w1_raw[1, 0], "vv")
+        d11 = round_weight(w1_raw[1, 1], "vv")
+        w1_q[1, 0] = quantise(d10, "w1q10")
+        w1_q[1, 1] = quantise(d11, "w1q11")
+        first_stage(1)
+
+        def pick(g, pos_t):
+            planes = work.tile([P, PACK, CUTS], BF16, name="planes", tag="planes%d" % g, bufs=1)
+            for t in range(PACK):
+                nc.vector.tensor_copy(out=planes[:, t, :], in_=h[g, t][:].indirect(pos_t[:]))
+            return planes
+
+        def weave(planes, eng="s"):
+            grouped = work.tile([P, CUTS * PACK], BF16, name="grouped", tag="grouped", bufs=2, align_bytes=64)
+            interleave(eng, grouped[:], planes[:])
+            return grouped
+
+        x1_q = {}
+        x2_q = {}
+        w3_q = {}
+        bent = {}
+        ghh = {}
+
+        def bend(g):
+            bent[g] = big.tile([P, PACK, CUTS], F32, name="bent", tag="big%d" % (4 + g))
+            for c in range(PACK):
+                n0 = g * GROUP + c * P
+                acc = psum.tile([P, CUTS], F32, name="bent_acc", tag="bank%d" % c)
+                for a in range(GROUPS):
+                    codes, scales = x1_q[a]
+                    nc.tensor.matmul_mx(
+                        out=acc[:],
+                        lhsT=w4_w[:, a, 2 * n0:2 * (n0 + P)].bitcast(FP4X4), lhsT_scale=w4_s[:, a, n0:n0 + P],
+                        rhs=codes[:].bitcast(FP8X4), rhs_scale=scales[:],
+                        start=(a == 0), stop=(a == GROUPS - 1))
+                rows = work.tile([P, CUTS], F32, name="bent_rows", tag="bent_rows", bufs=4)
+                nc.scalar.activation(out=rows[:], in_=acc[:], func=ACT.Tanh, bias=b2_t[:, g * PACK + c:g * PACK + c + 1])
+                nc.sync.dma_start(out=bent[g][32 * c:32 * (c + 1), :, :], in_=rows[:])
+
+        def scaled_h(g, c0, c1, slot):
+            out = big.tile([P, PACK, c1 - c0], F32, name="ghh", tag="big%d" % slot)
+            for t in range(PACK):
+                nc.scalar.activation(out=out[:, t, :], in_=h[g, t][:, c0:c1], func=ACT.Copy, scale=neg_gh[:, g, t:t + 1])
+            return out
+
+        p10 = pick(0, pos1_t)
+        p11 = pick(1, pos1_t)
+        g10 = weave(p10)
+        g11 = weave(p11)
+        x1_q[0] = quantise(g10, "x1q0")
+        p20 = pick(0, pos2_t)
+        x1_q[1] = quantise(g11, "x1q1")
+        d30 = round_weight(w3_raw[0, 0], "ss")
+        d31 = round_weight(w3_raw[0, 1], "ss")
+        g20 = weave(p20)
+        bend(0)
+        p21 = pick(1, pos2_t)
+        w3_q[0, 0] = quantise(d30, "w3q00")
+        w3_q[0, 1] = quantise(d31, "w3q01")
+        g21 = weave(p21, "v")
+        x2_q[0] = quantise(g20, "x2q0")
+        x2_q[1] = quantise(g21, "x2q1")
+
+        def second_stage(g):
+            cut = []
+            for t in range(PACK):
+                acc = psum.tile([P, CUTS], F32, name="cut_acc", tag="bank%d" % (PACK + t))
+                for a in range(GROUPS):
+                    w_codes, w_scales = w3_q[g, a]
+                    codes, scales = x2_q[a]
+                    nc.tensor.matmul_mx(
+                        out=acc[:],
+                        lhsT=w_codes[:, t * P:(t + 1) * P].bitcast(FP8X4), lhsT_scale=w_scales[:, t * P:(t + 1) * P],
+                        rhs=codes[:].bitcast(FP8X4), rhs_scale=scales[:],
+                        start=(a == 0), stop=(a == GROUPS - 1))
+                row = work.tile([P, CUTS], F32, name="cut", tag="cut", bufs=8)
+                nc.vector.scalar_tensor_tensor(out=row[:], in0=bent[g][:, t, :], scalar=amp_t[:, g, t:t + 1],
+                                               in1=acc[:], op0=ALU.mult, op1=ALU.add)
+                cut.append(row)
+            return cut
+
+        def spread(g, cut, c0, c1, slot):
+            n = c1 - c0
+            y = big.tile([P, PACK, n], F32, name="y", tag="big%d" % slot)
+            where = pos3_t[:, c0 // 16:c1 // 16]
+            for t in range(PACK):
+                if FUSED:
+                    nc.vector.tensor_tensor(out=y[:, t, :], in0=cut[t][:].indirect(where), in1=ghh[g, c0][:, t, :], op=ALU.add)
+                else:
+                    nc.vector.tensor_copy(out=y[:, t, :], in_=cut[t][:].indirect(where))
+            if not FUSED:
+                for t in range(PACK):
+                    nc.vector.scalar_tensor_tensor(out=y[:, t, :], in0=h[g, t][:, c0:c1], scalar=neg_gh[:, g, t:t + 1],
+                                                   in1=y[:, t, :], op0=ALU.mult, op1=ALU.add)
+            rows = out_0[g * GROUP:(g + 1) * GROUP, c0:c1].rearrange("(p t) j -> p t j", t=PACK)
+            nc.sync.dma_start(out=rows, in_=y[:])
+            return y
+
+        def round_y(y, eng):
+            n = y.shape[2]
+            grouped = work.tile([P, n * PACK], BF16, name="y_grouped", tag="y_grouped", bufs=2, align_bytes=64)
+            interleave(eng, grouped[:], y[:])
+            return grouped
+
+        def planes_out(g, grouped, y_s, c0, c1):
+            codes = work.tile([P, c1 - c0], U32, name="y_codes", tag="y_codes", align_bytes=64)
+            nc.vector.quantize_mx(out=codes[:].bitcast(FP8X4), scales=y_s[:, c0:c1], in_=grouped[:])
+            words = out_1[g].rearrange("p m t -> p (m t)").bitcast(I32)
+            nc.sync.dma_start(out=words[:, c0:c1], in_=codes[:].bitcast(I32))
+            if c1 == S:
+                for q in range(4):
+                    nc.scalar.dma_start(out=out_2[g, 4 * q:4 * q + 4, :].bitcast(I32),
+                                        in_=y_s[32 * q:32 * q + 4, :].bitcast(I32))
+
+        y_scales = [keep.tile([P, S], U8, name="y_s%d" % g, align_bytes=64) for g in range(GROUPS)]
+        steps = [(g, c0, c1) for g in range(GROUPS) for c0, c1 in SLICES]
+
+        def scale_step(step):
+            if FUSED and step < len(steps):
+                g, c0, c1 = steps[step]
+                ghh[g, c0] = scaled_h(g, c0, c1, 6 + step % 3)
+
+        scale_step(0)
+        cut = {0: second_stage(0)}
+        scale_step(1)
+        pending = None
+        for step, (g, c0, c1) in enumerate(steps):
+            if step == 3:
+                cut[1] = second_stage(1)
+            y = spread(g, cut[g], c0, c1, Y_SLOTS[step])
+            if pending is not None:
+                planes_out(*pending)
+            if step == 0:
+                bend(1)
+            if step < 2:
+                w3_q[1, step] = quantise(round_weight(w3_raw[1, step], "ss"), "w3q1%d" % step)
+            last = (g, c1) == (GROUPS - 1, S)
+            pending = (g, round_y(y, "v" if last else "s"), y_scales[g], c0, c1)
+            scale_step(step + 2)
+        planes_out(*pending)

@@ -22,7 +22,8 @@ GROUP = P * PACK
 GROUPS = 2
 BANK = 512
 SLICES = ((0, 384), (384, 768), (768, 1024))
-Y_SLOTS = (0, 1, 9, 0, 1, 9)
+Y_SLOTS = (0, 1, 6, 0, 1, 6)
+WIDE = 4 * 384
 FUSED = True
 
 
@@ -48,7 +49,7 @@ def tile_list_slab_bookmatch_features_kernel(
             return t
 
         def load_weight(w, g, a, slot, parts=1):
-            raw = big.tile([P, PACK, GROUP], F32, name="raw", tag="big%d" % slot)
+            raw = big.tile([P, PACK, GROUP], F32, name="raw", tag="big%d" % slot, align_bytes=64)
             rows = w[a * GROUP:(a + 1) * GROUP, g * GROUP:(g + 1) * GROUP]
             rows = rows.rearrange("(p j) c -> p j c", j=PACK)
             n = GROUP // parts
@@ -57,7 +58,7 @@ def tile_list_slab_bookmatch_features_kernel(
             return raw
 
         def load_table(a):
-            t = big.tile([P, T], I32, name="tabw", tag="big%d" % a)
+            t = big.tile([P, T], I32, name="tabw", tag="big%d" % a, align_bytes=64)
             nc.sync.dma_start(out=t[:], in_=tab_words[a].rearrange("p t i -> p (t i)").bitcast(I32))
             return t
 
@@ -67,17 +68,19 @@ def tile_list_slab_bookmatch_features_kernel(
             else:
                 nc.vector.tensor_copy(out=out, in_=in_)
 
-        def round_weight(raw, engines):
-            dealt = work.tile([P, GROUP * PACK], BF16, name="dealt", tag="dealt", align_bytes=64)
-            dst = dealt[:].rearrange("p (t m j) -> p m t j", t=PACK, j=PACK)
-            src = raw[:].rearrange("p j (m t) -> p m t j", t=PACK)
+        def round_weight(raw, engines, tag="dealt0", dealt=None):
+            if dealt is None:
+                dealt = big.tile([P, GROUP * PACK], BF16, name="dealt", tag=tag, align_bytes=64)
+            dst = dealt[:].rearrange("p (t m j) -> p m j t", t=PACK, j=PACK)
+            src = raw[:].rearrange("p j (m t) -> p m j t", t=PACK)
             half = P // 2
             for i, eng in enumerate(engines):
                 copy_on(eng, dst[:, i * half:(i + 1) * half], src[:, i * half:(i + 1) * half])
             return dealt
 
-        def quantise(grouped, name):
-            codes = keep.tile([P, GROUP], U32, name=name + "c", align_bytes=64)
+        def quantise(grouped, name, codes=None):
+            if codes is None:
+                codes = keep.tile([P, GROUP], U32, name=name + "c", align_bytes=64)
             scales = keep.tile([P, GROUP], U8, name=name + "s", align_bytes=64)
             nc.vector.quantize_mx(out=codes[:].bitcast(FP8X4), scales=scales[:], in_=grouped[:])
             return codes, scales
@@ -96,9 +99,10 @@ def tile_list_slab_bookmatch_features_kernel(
             nc.sync.dma_start(out=rows_s[32 * q:32 * q + 8, :], in_=tab_scales[:, 4 * q:4 * q + 4, :].bitcast(I32))
         for q in range(4):
             nc.vector.tensor_copy(out=tab_s[32 * q:32 * q + 8, :].bitcast(I32), in_=rows_s[32 * q:32 * q + 8, :])
-        tab_w = [load_table(0), load_table(1)]
         w1_raw = {}
+        tab_w = [load_table(0)]
         w1_raw[0, 0] = load_weight(w1, 0, 0, 2)
+        tab_w.append(load_table(1))
         w1_raw[0, 1] = load_weight(w1, 0, 1, 3, 2)
         b1_t = load_dealt(b1, "b1_t")
         gh_t = load_dealt(gh, "gh_t")
@@ -108,24 +112,24 @@ def tile_list_slab_bookmatch_features_kernel(
         pos2_t = load_list(pos2, "pos2_t")
         pos3_t = load_list(pos3, "pos3_t")
         amp_t = load_dealt(amp, "amp_t")
-        b2_t = keep.tile([P, H // P], F32, name="b2_t")
-        with nc.allow_non_contiguous_dma(reason="one bias value for each partition"):
-            nc.sync.dma_start(out=b2_t[:], in_=b2.rearrange("(c p) -> p c", p=P))
+        b2_t = []
+        for g in range(GROUPS):
+            t = big.tile([P, PACK], F32, name="b2_t", tag="late%d" % g, align_bytes=64)
+            with nc.allow_non_contiguous_dma(reason="one bias value for each partition"):
+                nc.sync.dma_start(out=t[:], in_=b2[g * GROUP:(g + 1) * GROUP].rearrange("(c p) -> p c", p=P))
+            b2_t.append(t)
         for q in range(4):
             nc.sync.dma_start(out=w4_s[32 * q:32 * q + 4, :, :].bitcast(I32),
                               in_=w4_scales[:, 4 * q:4 * q + 4, :].rearrange("a q c -> q a c").bitcast(I32))
         w4_w = keep.tile([P, GROUPS, 2 * H], U8, name="w4_w", align_bytes=64)
         nc.sync.dma_start(out=w4_w[:].bitcast(I32), in_=w4_words.rearrange("a p c -> p a c").bitcast(I32))
-        w3_raw = {}
-        for g in range(GROUPS):
-            for a in range(GROUPS):
-                w3_raw[g, a] = load_weight(w3, g, a, 2 * g + a)
+        w3_raw = {(1, a): load_weight(w3, 1, a, 2 + a) for a in range(GROUPS)}
 
-        v_s = keep.tile([P, S], U8, name="v_s", align_bytes=64)
+        v_s = big.tile([P, S], U8, name="v_s", tag="grouped0", align_bytes=64)
         nc.vector.tensor_copy(out=v_s[:], in_=tab_s[:].indirect(offs_t[:]))
         v_w = []
         for a in range(GROUPS):
-            t = keep.tile([P, S], U32, name="v_w%d" % a, align_bytes=64)
+            t = big.tile([P, S], U32, name="v_w%d" % a, tag="big%d" % (6 + a), align_bytes=64)
             nc.vector.tensor_copy(out=t[:], in_=tab_w[a][:].bitcast(U32).indirect(offs_t[:]))
             v_w.append(t)
 
@@ -151,25 +155,29 @@ def tile_list_slab_bookmatch_features_kernel(
                                          bias=b1_t[:, g, t:t + 1])
 
         d00 = round_weight(w1_raw[0, 0], "ss")
-        d01 = round_weight(w1_raw[0, 1], "sv")
+        d01 = round_weight(w1_raw[0, 1], "sv", "dealt1")
         w1_q[0, 0] = quantise(d00, "w1q00")
         w1_q[0, 1] = quantise(d01, "w1q01")
         first_stage(0)
-        d10 = round_weight(w1_raw[1, 0], "vv")
-        d11 = round_weight(w1_raw[1, 1], "vv")
+        d10 = round_weight(w1_raw[1, 0], "vv", "dealt2")
+        d11 = round_weight(w1_raw[1, 1], "vv", "dealt0")
         w1_q[1, 0] = quantise(d10, "w1q10")
         w1_q[1, 1] = quantise(d11, "w1q11")
         first_stage(1)
+        for a in range(GROUPS):
+            w3_raw[0, a] = load_weight(w3, 0, a, 6 + a)
 
         def pick(g, pos_t):
-            planes = work.tile([P, PACK, CUTS], BF16, name="planes", tag="planes%d" % g, bufs=1)
+            planes = big.tile([P, PACK, CUTS], BF16, name="planes", tag="planes%d" % g, align_bytes=64)
             for t in range(PACK):
                 nc.vector.tensor_copy(out=planes[:, t, :], in_=h[g, t][:].indirect(pos_t[:]))
             return planes
 
-        def weave(planes, eng="s"):
-            grouped = work.tile([P, CUTS * PACK], BF16, name="grouped", tag="grouped", bufs=2, align_bytes=64)
-            interleave(eng, grouped[:], planes[:])
+        def weave(planes, engines, tag):
+            grouped = big.tile([P, CUTS * PACK], BF16, name="grouped", tag=tag, align_bytes=64)
+            n = CUTS // len(engines)
+            for i, eng in enumerate(engines):
+                interleave(eng, grouped[:, i * n * PACK:(i + 1) * n * PACK], planes[:, :, i * n:(i + 1) * n])
             return grouped
 
         x1_q = {}
@@ -178,11 +186,11 @@ def tile_list_slab_bookmatch_features_kernel(
         bent = {}
         ghh = {}
 
-        def bend(g):
-            bent[g] = big.tile([P, PACK, CUTS], F32, name="bent", tag="big%d" % (4 + g))
+        def bend(g, together):
+            bent[g] = big.tile([P, PACK, CUTS], F32, name="bent", tag="big%d" % (4 + g), align_bytes=64)
             for c in range(PACK):
                 n0 = g * GROUP + c * P
-                acc = psum.tile([P, CUTS], F32, name="bent_acc", tag="bank%d" % c)
+                acc = psum.tile([P, CUTS], F32, name="bent_acc", tag="bank%d" % (PACK * g + c))
                 for a in range(GROUPS):
                     codes, scales = x1_q[a]
                     nc.tensor.matmul_mx(
@@ -190,38 +198,40 @@ def tile_list_slab_bookmatch_features_kernel(
                         lhsT=w4_w[:, a, 2 * n0:2 * (n0 + P)].bitcast(FP4X4), lhsT_scale=w4_s[:, a, n0:n0 + P],
                         rhs=codes[:].bitcast(FP8X4), rhs_scale=scales[:],
                         start=(a == 0), stop=(a == GROUPS - 1))
-                rows = work.tile([P, CUTS], F32, name="bent_rows", tag="bent_rows", bufs=4)
-                nc.scalar.activation(out=rows[:], in_=acc[:], func=ACT.Tanh, bias=b2_t[:, g * PACK + c:g * PACK + c + 1])
-                nc.sync.dma_start(out=bent[g][32 * c:32 * (c + 1), :, :], in_=rows[:])
+                rows = together[:, PACK * g + c, :]
+                nc.scalar.activation(out=rows, in_=acc[:], func=ACT.Tanh, bias=b2_t[g][:, c:c + 1])
+                nc.sync.dma_start(out=bent[g][32 * c:32 * (c + 1), :, :], in_=rows)
 
         def scaled_h(g, c0, c1, slot):
-            out = big.tile([P, PACK, c1 - c0], F32, name="ghh", tag="big%d" % slot)
+            out = late[:, slot * WIDE:slot * WIDE + PACK * (c1 - c0)].rearrange("p (t c) -> p t c", t=PACK)
             for t in range(PACK):
                 nc.scalar.activation(out=out[:, t, :], in_=h[g, t][:, c0:c1], func=ACT.Copy, scale=neg_gh[:, g, t:t + 1])
             return out
 
         p10 = pick(0, pos1_t)
         p11 = pick(1, pos1_t)
-        g10 = weave(p10)
-        g11 = weave(p11)
+        g10 = weave(p10, "s", "grouped0")
+        g11 = weave(p11, "s", "grouped1")
         x1_q[0] = quantise(g10, "x1q0")
         p20 = pick(0, pos2_t)
         x1_q[1] = quantise(g11, "x1q1")
-        d30 = round_weight(w3_raw[0, 0], "ss")
-        d31 = round_weight(w3_raw[0, 1], "ss")
-        g20 = weave(p20)
-        bend(0)
+        d30 = round_weight(w3_raw[0, 0], "ss", "dealt1")
+        d31 = round_weight(w3_raw[0, 1], "ss", "dealt2")
+        g20 = weave(p20, "s", "big7")
+        bent_rows = big.tile([P, GROUPS * PACK, CUTS], F32, name="bent_rows", tag="planes0", align_bytes=64)
+        bend(0, bent_rows)
+        bend(1, bent_rows)
         p21 = pick(1, pos2_t)
         w3_q[0, 0] = quantise(d30, "w3q00")
         w3_q[0, 1] = quantise(d31, "w3q01")
-        g21 = weave(p21, "v")
         x2_q[0] = quantise(g20, "x2q0")
+        g21 = weave(p21, "v", "big7")
         x2_q[1] = quantise(g21, "x2q1")
 
         def second_stage(g):
             cut = []
             for t in range(PACK):
-                acc = psum.tile([P, CUTS], F32, name="cut_acc", tag="bank%d" % (PACK + t))
+                acc = psum.tile([P, CUTS], F32, name="cut_acc", tag="bank%d" % (PACK * g + t))
                 for a in range(GROUPS):
                     w_codes, w_scales = w3_q[g, a]
                     codes, scales = x2_q[a]
@@ -238,7 +248,7 @@ def tile_list_slab_bookmatch_features_kernel(
 
         def spread(g, cut, c0, c1, slot):
             n = c1 - c0
-            y = big.tile([P, PACK, n], F32, name="y", tag="big%d" % slot)
+            y = big.tile([P, PACK, n], F32, name="y", tag="big%d" % slot, align_bytes=64)
             where = pos3_t[:, c0 // 16:c1 // 16]
             for t in range(PACK):
                 if FUSED:
@@ -253,7 +263,7 @@ def tile_list_slab_bookmatch_features_kernel(
             nc.sync.dma_start(out=rows, in_=y[:])
             return y
 
-        def round_y(y, eng):
+        def round_y(y, eng, step):
             n = y.shape[2]
             grouped = work.tile([P, n * PACK], BF16, name="y_grouped", tag="y_grouped", bufs=2, align_bytes=64)
             interleave(eng, grouped[:], y[:])
@@ -261,37 +271,42 @@ def tile_list_slab_bookmatch_features_kernel(
 
         def planes_out(g, grouped, y_s, c0, c1):
             codes = work.tile([P, c1 - c0], U32, name="y_codes", tag="y_codes", align_bytes=64)
-            nc.vector.quantize_mx(out=codes[:].bitcast(FP8X4), scales=y_s[:, c0:c1], in_=grouped[:])
+            nc.vector.quantize_mx(out=codes[:].bitcast(FP8X4), scales=y_s[:, g, c0:c1], in_=grouped[:])
             words = out_1[g].rearrange("p m t -> p (m t)").bitcast(I32)
             nc.sync.dma_start(out=words[:, c0:c1], in_=codes[:].bitcast(I32))
-            if c1 == S:
-                for q in range(4):
-                    nc.scalar.dma_start(out=out_2[g, 4 * q:4 * q + 4, :].bitcast(I32),
-                                        in_=y_s[32 * q:32 * q + 4, :].bitcast(I32))
 
-        y_scales = [keep.tile([P, S], U8, name="y_s%d" % g, align_bytes=64) for g in range(GROUPS)]
+        y_scales = keep.tile([P, GROUPS, S], U8, name="y_s", align_bytes=64)
         steps = [(g, c0, c1) for g in range(GROUPS) for c0, c1 in SLICES]
 
         def scale_step(step):
             if FUSED and step < len(steps):
                 g, c0, c1 = steps[step]
-                ghh[g, c0] = scaled_h(g, c0, c1, 6 + step % 3)
+                ghh[g, c0] = scaled_h(g, c0, c1, step % 3)
 
+        late = big.tile([P, 3 * WIDE], F32, name="late", tag="late0", align_bytes=64)
+        late_pair = big.tile([P, 2 * PACK * GROUP], BF16, name="late_pair", tag="late1", align_bytes=64)
+        late_bf16 = [late_pair[:, PACK * GROUP * a:PACK * GROUP * (a + 1)] for a in range(2)]
         scale_step(0)
         cut = {0: second_stage(0)}
         scale_step(1)
+        for a in range(GROUPS):
+            round_weight(w3_raw[1, a], "ss", dealt=late_bf16[a])
+        scale_step(2)
         pending = None
         for step, (g, c0, c1) in enumerate(steps):
             if step == 3:
                 cut[1] = second_stage(1)
             y = spread(g, cut[g], c0, c1, Y_SLOTS[step])
+            if step == 1:
+                both = big.tile([P, GROUPS * GROUP], U32, name="w3q1c", tag="big4", align_bytes=64)
+                for a in range(GROUPS):
+                    w3_q[1, a] = quantise(late_bf16[a], "w3q1%d" % a, both[:, a * GROUP:(a + 1) * GROUP])
             if pending is not None:
                 planes_out(*pending)
-            if step == 0:
-                bend(1)
-            if step < 2:
-                w3_q[1, step] = quantise(round_weight(w3_raw[1, step], "ss"), "w3q1%d" % step)
             last = (g, c1) == (GROUPS - 1, S)
-            pending = (g, round_y(y, "v" if last else "s"), y_scales[g], c0, c1)
-            scale_step(step + 2)
+            pending = (g, round_y(y, "v" if last else "s", step), y_scales, c0, c1)
+            scale_step(step + 3)
         planes_out(*pending)
+        for q in range(4):
+            nc.scalar.dma_start(out=out_2[:, 4 * q:4 * q + 4, :].rearrange("g r c -> r g c").bitcast(I32),
+                                in_=y_scales[32 * q:32 * q + 4, :, :].bitcast(I32))

@@ -24,6 +24,7 @@ BANK = 512
 SLICES = ((0, 384), (384, 768), (768, 1024))
 Y_SLOTS = (0, 1, 6, 0, 1, 6)
 WIDE = 4 * 384
+LAG = 2
 FUSED = True
 
 
@@ -71,8 +72,8 @@ def tile_list_slab_bookmatch_features_kernel(
         def round_weight(raw, engines, tag="dealt0", dealt=None):
             if dealt is None:
                 dealt = big.tile([P, GROUP * PACK], BF16, name="dealt", tag=tag, align_bytes=64)
-            dst = dealt[:].rearrange("p (t m j) -> p m j t", t=PACK, j=PACK)
-            src = raw[:].rearrange("p j (m t) -> p m j t", t=PACK)
+            dst = dealt[:].rearrange("p (t m j) -> p m t j", t=PACK, j=PACK)
+            src = raw[:].rearrange("p j (m t) -> p m t j", t=PACK)
             half = P // 2
             for i, eng in enumerate(engines):
                 copy_on(eng, dst[:, i * half:(i + 1) * half], src[:, i * half:(i + 1) * half])
@@ -165,7 +166,7 @@ def tile_list_slab_bookmatch_features_kernel(
         w1_q[1, 1] = quantise(d11, "w1q11")
         first_stage(1)
         for a in range(GROUPS):
-            w3_raw[0, a] = load_weight(w3, 0, a, 6 + a)
+            w3_raw[0, 1 - a] = load_weight(w3, 0, 1 - a, 6 + a)
 
         def pick(g, pos_t):
             planes = big.tile([P, PACK, CUTS], BF16, name="planes", tag="planes%d" % g, align_bytes=64)
@@ -186,7 +187,8 @@ def tile_list_slab_bookmatch_features_kernel(
         bent = {}
         ghh = {}
 
-        def bend(g, together):
+        def bend(g, tag):
+            together = big.tile([P, PACK, CUTS], F32, name="bent_rows", tag=tag, align_bytes=64)
             bent[g] = big.tile([P, PACK, CUTS], F32, name="bent", tag="big%d" % (4 + g), align_bytes=64)
             for c in range(PACK):
                 n0 = g * GROUP + c * P
@@ -198,7 +200,7 @@ def tile_list_slab_bookmatch_features_kernel(
                         lhsT=w4_w[:, a, 2 * n0:2 * (n0 + P)].bitcast(FP4X4), lhsT_scale=w4_s[:, a, n0:n0 + P],
                         rhs=codes[:].bitcast(FP8X4), rhs_scale=scales[:],
                         start=(a == 0), stop=(a == GROUPS - 1))
-                rows = together[:, PACK * g + c, :]
+                rows = together[:, c, :]
                 nc.scalar.activation(out=rows, in_=acc[:], func=ACT.Tanh, bias=b2_t[g][:, c:c + 1])
                 nc.sync.dma_start(out=bent[g][32 * c:32 * (c + 1), :, :], in_=rows)
 
@@ -215,31 +217,30 @@ def tile_list_slab_bookmatch_features_kernel(
         x1_q[0] = quantise(g10, "x1q0")
         p20 = pick(0, pos2_t)
         x1_q[1] = quantise(g11, "x1q1")
-        d30 = round_weight(w3_raw[0, 0], "ss", "dealt1")
-        d31 = round_weight(w3_raw[0, 1], "ss", "dealt2")
-        g20 = weave(p20, "s", "big7")
-        bent_rows = big.tile([P, GROUPS * PACK, CUTS], F32, name="bent_rows", tag="planes0", align_bytes=64)
-        bend(0, bent_rows)
-        bend(1, bent_rows)
+        d31 = round_weight(w3_raw[0, 1], "ss", "dealt1")
+        d30 = round_weight(w3_raw[0, 0], "ss", "dealt2")
+        bend(0, "big7")
+        g20 = weave(p20, "s", "late0")
+        bend(1, "planes0")
         p21 = pick(1, pos2_t)
-        w3_q[0, 0] = quantise(d30, "w3q00")
         w3_q[0, 1] = quantise(d31, "w3q01")
-        x2_q[0] = quantise(g20, "x2q0")
-        g21 = weave(p21, "v", "big7")
+        w3_q[0, 0] = quantise(d30, "w3q00")
+        g21 = weave(p21, "v", "grouped0")
         x2_q[1] = quantise(g21, "x2q1")
+        x2_q[0] = quantise(g20, "x2q0")
 
         def second_stage(g):
             cut = []
             for t in range(PACK):
                 acc = psum.tile([P, CUTS], F32, name="cut_acc", tag="bank%d" % (PACK * g + t))
-                for a in range(GROUPS):
+                for a in (1, 0):
                     w_codes, w_scales = w3_q[g, a]
                     codes, scales = x2_q[a]
                     nc.tensor.matmul_mx(
                         out=acc[:],
                         lhsT=w_codes[:, t * P:(t + 1) * P].bitcast(FP8X4), lhsT_scale=w_scales[:, t * P:(t + 1) * P],
                         rhs=codes[:].bitcast(FP8X4), rhs_scale=scales[:],
-                        start=(a == 0), stop=(a == GROUPS - 1))
+                        start=(a == 1), stop=(a == 0))
                 row = work.tile([P, CUTS], F32, name="cut", tag="cut", bufs=8)
                 nc.vector.scalar_tensor_tensor(out=row[:], in0=bent[g][:, t, :], scalar=amp_t[:, g, t:t + 1],
                                                in1=acc[:], op0=ALU.mult, op1=ALU.add)
@@ -265,7 +266,7 @@ def tile_list_slab_bookmatch_features_kernel(
 
         def round_y(y, eng, step):
             n = y.shape[2]
-            grouped = work.tile([P, n * PACK], BF16, name="y_grouped", tag="y_grouped", bufs=2, align_bytes=64)
+            grouped = work.tile([P, n * PACK], BF16, name="y_grouped", tag="y_grouped", bufs=3, align_bytes=64)
             interleave(eng, grouped[:], y[:])
             return grouped
 
@@ -283,8 +284,8 @@ def tile_list_slab_bookmatch_features_kernel(
                 g, c0, c1 = steps[step]
                 ghh[g, c0] = scaled_h(g, c0, c1, step % 3)
 
-        late = big.tile([P, 3 * WIDE], F32, name="late", tag="late0", align_bytes=64)
-        late_pair = big.tile([P, 2 * PACK * GROUP], BF16, name="late_pair", tag="late1", align_bytes=64)
+        late = big.tile([P, 3 * WIDE], F32, name="late", tag="late1", align_bytes=64)
+        late_pair = big.tile([P, 2 * PACK * GROUP], BF16, name="late_pair", tag="late0", align_bytes=64)
         late_bf16 = [late_pair[:, PACK * GROUP * a:PACK * GROUP * (a + 1)] for a in range(2)]
         scale_step(0)
         cut = {0: second_stage(0)}
@@ -292,7 +293,7 @@ def tile_list_slab_bookmatch_features_kernel(
         for a in range(GROUPS):
             round_weight(w3_raw[1, a], "ss", dealt=late_bf16[a])
         scale_step(2)
-        pending = None
+        pending = []
         for step, (g, c0, c1) in enumerate(steps):
             if step == 3:
                 cut[1] = second_stage(1)
@@ -301,12 +302,13 @@ def tile_list_slab_bookmatch_features_kernel(
                 both = big.tile([P, GROUPS * GROUP], U32, name="w3q1c", tag="big4", align_bytes=64)
                 for a in range(GROUPS):
                     w3_q[1, a] = quantise(late_bf16[a], "w3q1%d" % a, both[:, a * GROUP:(a + 1) * GROUP])
-            if pending is not None:
-                planes_out(*pending)
+            if len(pending) == LAG:
+                planes_out(*pending.pop(0))
             last = (g, c1) == (GROUPS - 1, S)
-            pending = (g, round_y(y, "v" if last else "s", step), y_scales, c0, c1)
+            pending.append((g, round_y(y, "v" if last else "s", step), y_scales, c0, c1))
             scale_step(step + 3)
-        planes_out(*pending)
+        for item in pending:
+            planes_out(*item)
         for q in range(4):
             nc.scalar.dma_start(out=out_2[:, 4 * q:4 * q + 4, :].rearrange("g r c -> r g c").bitcast(I32),
                                 in_=y_scales[32 * q:32 * q + 4, :, :].bitcast(I32))

@@ -106,13 +106,13 @@ def tile_list_slab_bookmatch_features_kernel(
         tab_w.append(load_table(1))
         w1_raw[0, 1] = load_weight(w1, 0, 1, 3, 2)
         b1_t = load_dealt(b1, "b1_t")
-        gh_t = load_dealt(gh, "gh_t")
         w1_raw[1, 0] = load_weight(w1, 1, 0, 4)
         w1_raw[1, 1] = load_weight(w1, 1, 1, 5)
         pos1_t = load_list(pos1, "pos1_t")
         pos2_t = load_list(pos2, "pos2_t")
         pos3_t = load_list(pos3, "pos3_t")
         amp_t = load_dealt(amp, "amp_t")
+        gh_t = load_dealt(gh, "gh_t")
         b2_t = []
         for g in range(GROUPS):
             t = big.tile([P, PACK], F32, name="b2_t", tag="late%d" % g, align_bytes=64)
@@ -160,7 +160,7 @@ def tile_list_slab_bookmatch_features_kernel(
         w1_q[0, 0] = quantise(d00, "w1q00")
         w1_q[0, 1] = quantise(d01, "w1q01")
         first_stage(0)
-        d10 = round_weight(w1_raw[1, 0], "vv", "dealt2")
+        d10 = round_weight(w1_raw[1, 0], "sv", "dealt2")
         d11 = round_weight(w1_raw[1, 1], "vv", "dealt0")
         w1_q[1, 0] = quantise(d10, "w1q10")
         w1_q[1, 1] = quantise(d11, "w1q11")
@@ -190,7 +190,7 @@ def tile_list_slab_bookmatch_features_kernel(
         def bend(g, tag):
             together = big.tile([P, PACK, CUTS], F32, name="bent_rows", tag=tag, align_bytes=64)
             bent[g] = big.tile([P, PACK, CUTS], F32, name="bent", tag="big%d" % (4 + g), align_bytes=64)
-            for c in range(PACK):
+            for c in (0, 2, 1, 3):
                 n0 = g * GROUP + c * P
                 acc = psum.tile([P, CUTS], F32, name="bent_acc", tag="bank%d" % (PACK * g + c))
                 for a in range(GROUPS):
@@ -252,14 +252,11 @@ def tile_list_slab_bookmatch_features_kernel(
             y = big.tile([P, PACK, n], F32, name="y", tag="big%d" % slot, align_bytes=64)
             where = pos3_t[:, c0 // 16:c1 // 16]
             for t in range(PACK):
-                if FUSED:
+                if (g, c1) == (GROUPS - 1, S):
                     nc.vector.tensor_tensor(out=y[:, t, :], in0=cut[t][:].indirect(where), in1=ghh[g, c0][:, t, :], op=ALU.add)
                 else:
                     nc.vector.tensor_copy(out=y[:, t, :], in_=cut[t][:].indirect(where))
-            if not FUSED:
-                for t in range(PACK):
-                    nc.vector.scalar_tensor_tensor(out=y[:, t, :], in0=h[g, t][:, c0:c1], scalar=neg_gh[:, g, t:t + 1],
-                                                   in1=y[:, t, :], op0=ALU.mult, op1=ALU.add)
+                    nc.gpsimd.tensor_tensor(out=y[:, t, :], in0=y[:, t, :], in1=ghh[g, c0][:, t, :], op=ALU.add)
             rows = out_0[g * GROUP:(g + 1) * GROUP, c0:c1].rearrange("(p t) j -> p t j", t=PACK)
             nc.sync.dma_start(out=rows, in_=y[:])
             return y
@@ -267,7 +264,9 @@ def tile_list_slab_bookmatch_features_kernel(
         def round_y(y, eng, step):
             n = y.shape[2]
             grouped = work.tile([P, n * PACK], BF16, name="y_grouped", tag="y_grouped", bufs=3, align_bytes=64)
-            interleave(eng, grouped[:], y[:])
+            part = n // len(eng)
+            for i, e in enumerate(eng):
+                interleave(e, grouped[:, i * part * PACK:(i + 1) * part * PACK], y[:, :, i * part:(i + 1) * part])
             return grouped
 
         def planes_out(g, grouped, y_s, c0, c1):
@@ -284,7 +283,7 @@ def tile_list_slab_bookmatch_features_kernel(
                 g, c0, c1 = steps[step]
                 ghh[g, c0] = scaled_h(g, c0, c1, step % 3)
 
-        late = big.tile([P, 3 * WIDE], F32, name="late", tag="late1", align_bytes=64)
+        late = big.tile([P, 3 * WIDE], F32, name="late", tag="late1", align_bytes=64) if FUSED else None
         late_pair = big.tile([P, 2 * PACK * GROUP], BF16, name="late_pair", tag="late0", align_bytes=64)
         late_bf16 = [late_pair[:, PACK * GROUP * a:PACK * GROUP * (a + 1)] for a in range(2)]
         scale_step(0)

@@ -20,12 +20,18 @@ P = 128
 PACK = 4
 GROUP = P * PACK
 GROUPS = 2
+QUADRANTS = 4
+QUAD = P // QUADRANTS
+SCALE_ROWS = 4
 BANK = 512
-SLICES = ((0, 384), (384, 768), (768, 1024))
-Y_SLOTS = (0, 1, 6, 0, 1, 6)
-WIDE = 4 * 384
+PER_COLUMN = 16
+ALIGN = 64
+RUN = 4
+SPANS = ((0, 384), (384, 768), (768, 1024))
+SPAN_MAX = 384
+RING = 3
+Y_TAGS = ("tab0", "tab1", "v0")
 LAG = 2
-FUSED = True
 
 
 def tile_list_slab_bookmatch_features_kernel(
@@ -35,79 +41,96 @@ def tile_list_slab_bookmatch_features_kernel(
     nc = tc.nc
     with ExitStack() as ctx:
         keep = ctx.enter_context(tc.tile_pool(name="keep", bufs=1))
-        big = ctx.enter_context(tc.tile_pool(name="big", bufs=1))
-        work = ctx.enter_context(tc.tile_pool(name="work", bufs=3))
+        slots = ctx.enter_context(tc.tile_pool(name="slots", bufs=1))
+        work = ctx.enter_context(tc.tile_pool(name="work", bufs=RING))
         psum = ctx.enter_context(tc.psum_pool(name="psum", bufs=1))
 
+        def on_scalar(out, in_):
+            nc.scalar.copy(out=out, in_=in_)
+
+        def on_vector(out, in_):
+            nc.vector.tensor_copy(out=out, in_=in_)
+
+        def slot(shape, dtype, name, tag):
+            return slots.tile(shape, dtype, name=name, tag=tag, align_bytes=ALIGN)
+
+        def quadrant(q, rows):
+            return slice(QUAD * q, QUAD * q + rows)
+
+        def scale_rows(q):
+            return slice(SCALE_ROWS * q, SCALE_ROWS * (q + 1))
+
         def load_list(src, name):
-            t = keep.tile(list(src.shape), U16, name=name)
-            nc.sync.dma_start(out=t[:], in_=src)
-            return t
+            tile = keep.tile(list(src.shape), U16, name=name)
+            nc.sync.dma_start(out=tile[:], in_=src)
+            return tile
 
         def load_dealt(vec, name):
-            t = keep.tile([P, GROUPS, PACK], F32, name=name)
-            nc.sync.dma_start(out=t[:], in_=vec.rearrange("(g p t) -> p g t", g=GROUPS, t=PACK))
-            return t
+            tile = keep.tile([P, GROUPS, PACK], F32, name=name)
+            nc.sync.dma_start(out=tile[:], in_=vec.rearrange("(g p t) -> p g t", g=GROUPS, t=PACK))
+            return tile
 
-        def load_weight(w, g, a, slot, parts=1):
-            raw = big.tile([P, PACK, GROUP], F32, name="raw", tag="big%d" % slot, align_bytes=64)
-            rows = w[a * GROUP:(a + 1) * GROUP, g * GROUP:(g + 1) * GROUP]
-            rows = rows.rearrange("(p j) c -> p j c", j=PACK)
-            n = GROUP // parts
+        def load_weight(w, g, a, tag, parts=1):
+            raw = slot([P, PACK, GROUP], F32, "raw", tag)
+            rows = w[a * GROUP:(a + 1) * GROUP, g * GROUP:(g + 1) * GROUP].rearrange("(p j) c -> p j c", j=PACK)
+            width = GROUP // parts
             for i in range(parts):
-                nc.sync.dma_start(out=raw[:, :, i * n:(i + 1) * n], in_=rows[:, :, i * n:(i + 1) * n])
+                cols = slice(i * width, (i + 1) * width)
+                nc.sync.dma_start(out=raw[:, :, cols], in_=rows[:, :, cols])
             return raw
 
         def load_table(a):
-            t = big.tile([P, T], I32, name="tabw", tag="big%d" % a, align_bytes=64)
-            nc.sync.dma_start(out=t[:], in_=tab_words[a].rearrange("p t i -> p (t i)").bitcast(I32))
-            return t
+            tile = slot([P, T], I32, "tab_w", "tab%d" % a)
+            nc.sync.dma_start(out=tile[:], in_=tab_words[a].rearrange("p t i -> p (t i)").bitcast(I32))
+            return tile
 
-        def copy_on(eng, out, in_):
-            if eng == "s":
-                nc.scalar.copy(out=out, in_=in_)
-            else:
-                nc.vector.tensor_copy(out=out, in_=in_)
-
-        def round_weight(raw, engines, tag="dealt0", dealt=None):
-            if dealt is None:
-                dealt = big.tile([P, GROUP * PACK], BF16, name="dealt", tag=tag, align_bytes=64)
-            dst = dealt[:].rearrange("p (t m j) -> p m t j", t=PACK, j=PACK)
+        def round_weight(raw, rounded, copies):
+            dst = rounded[:].rearrange("p (t m j) -> p m t j", t=PACK, j=PACK)
             src = raw[:].rearrange("p j (m t) -> p m t j", t=PACK)
             half = P // 2
-            for i, eng in enumerate(engines):
-                copy_on(eng, dst[:, i * half:(i + 1) * half], src[:, i * half:(i + 1) * half])
-            return dealt
+            for i, copy in enumerate(copies):
+                copy(dst[:, i * half:(i + 1) * half], src[:, i * half:(i + 1) * half])
+            return rounded
 
-        def quantise(grouped, name, codes=None):
-            if codes is None:
-                codes = keep.tile([P, GROUP], U32, name=name + "c", align_bytes=64)
-            scales = keep.tile([P, GROUP], U8, name=name + "s", align_bytes=64)
-            nc.vector.quantize_mx(out=codes[:].bitcast(FP8X4), scales=scales[:], in_=grouped[:])
+        def rounded_slot(tag):
+            return slot([P, GROUP * PACK], BF16, "rounded", tag)
+
+        def quantise_into(codes, values, name):
+            scales = keep.tile([P, GROUP], U8, name=name + "_scales", align_bytes=ALIGN)
+            nc.vector.quantize_mx(out=codes[:].bitcast(FP8X4), scales=scales[:], in_=values[:])
             return codes, scales
 
-        def interleave(eng, out, planes):
-            copy_on(eng, out.rearrange("p (c i t) -> p c t i", i=4, t=PACK),
-                    planes.rearrange("p t (c i) -> p c t i", i=4))
+        def quantise(values, name):
+            return quantise_into(keep.tile([P, GROUP], U32, name=name + "_codes", align_bytes=ALIGN), values, name)
+
+        def interleave(woven, planes, copies):
+            share = planes.shape[2] // len(copies)
+            for i, copy in enumerate(copies):
+                dst = woven[:, i * share * PACK:(i + 1) * share * PACK]
+                src = planes[:, :, i * share:(i + 1) * share]
+                copy(dst.rearrange("p (c i t) -> p c t i", i=RUN, t=PACK), src.rearrange("p t (c i) -> p c t i", i=RUN))
+            return woven
 
         tab_s = keep.tile([P, T], U8, name="tab_s")
-        w4_s = keep.tile([P, GROUPS, H], U8, name="w4_s", align_bytes=64)
+        w4_s = keep.tile([P, GROUPS, H], U8, name="w4_s", align_bytes=ALIGN)
         nc.vector.memset(tab_s[:].bitcast(I32), 0)
         nc.gpsimd.memset(w4_s[:].bitcast(I32), 0)
         offs_t = load_list(offs, "offs_t")
-        rows_s = keep.tile([P, T // 4], I32, name="rows_s")
-        for q in range(4):
-            nc.sync.dma_start(out=rows_s[32 * q:32 * q + 8, :], in_=tab_scales[:, 4 * q:4 * q + 4, :].bitcast(I32))
-        for q in range(4):
-            nc.vector.tensor_copy(out=tab_s[32 * q:32 * q + 8, :].bitcast(I32), in_=rows_s[32 * q:32 * q + 8, :])
+        staged_s = keep.tile([P, T // 4], I32, name="staged_s")
+        for q in range(QUADRANTS):
+            nc.sync.dma_start(out=staged_s[quadrant(q, GROUPS * SCALE_ROWS), :],
+                              in_=tab_scales[:, scale_rows(q), :].bitcast(I32))
+        for q in range(QUADRANTS):
+            live = quadrant(q, GROUPS * SCALE_ROWS)
+            nc.vector.tensor_copy(out=tab_s[live, :].bitcast(I32), in_=staged_s[live, :])
         w1_raw = {}
         tab_w = [load_table(0)]
-        w1_raw[0, 0] = load_weight(w1, 0, 0, 2)
+        w1_raw[0, 0] = load_weight(w1, 0, 0, "w00")
         tab_w.append(load_table(1))
-        w1_raw[0, 1] = load_weight(w1, 0, 1, 3, 2)
+        w1_raw[0, 1] = load_weight(w1, 0, 1, "w01", parts=2)
         b1_t = load_dealt(b1, "b1_t")
-        w1_raw[1, 0] = load_weight(w1, 1, 0, 4)
-        w1_raw[1, 1] = load_weight(w1, 1, 1, 5)
+        w1_raw[1, 0] = load_weight(w1, 1, 0, "w10")
+        w1_raw[1, 1] = load_weight(w1, 1, 1, "w11")
         pos1_t = load_list(pos1, "pos1_t")
         pos2_t = load_list(pos2, "pos2_t")
         pos3_t = load_list(pos3, "pos3_t")
@@ -115,24 +138,24 @@ def tile_list_slab_bookmatch_features_kernel(
         gh_t = load_dealt(gh, "gh_t")
         b2_t = []
         for g in range(GROUPS):
-            t = big.tile([P, PACK], F32, name="b2_t", tag="late%d" % g, align_bytes=64)
+            bias = slot([P, PACK], F32, "b2_t", "bias%d" % g)
             with nc.allow_non_contiguous_dma(reason="one bias value for each partition"):
-                nc.sync.dma_start(out=t[:], in_=b2[g * GROUP:(g + 1) * GROUP].rearrange("(c p) -> p c", p=P))
-            b2_t.append(t)
-        for q in range(4):
-            nc.sync.dma_start(out=w4_s[32 * q:32 * q + 4, :, :].bitcast(I32),
-                              in_=w4_scales[:, 4 * q:4 * q + 4, :].rearrange("a q c -> q a c").bitcast(I32))
-        w4_w = keep.tile([P, GROUPS, 2 * H], U8, name="w4_w", align_bytes=64)
+                nc.sync.dma_start(out=bias[:], in_=b2[g * GROUP:(g + 1) * GROUP].rearrange("(c p) -> p c", p=P))
+            b2_t.append(bias)
+        for q in range(QUADRANTS):
+            nc.sync.dma_start(out=w4_s[quadrant(q, SCALE_ROWS), :, :].bitcast(I32),
+                              in_=w4_scales[:, scale_rows(q), :].rearrange("a r c -> r a c").bitcast(I32))
+        w4_w = keep.tile([P, GROUPS, 2 * H], U8, name="w4_w", align_bytes=ALIGN)
         nc.sync.dma_start(out=w4_w[:].bitcast(I32), in_=w4_words.rearrange("a p c -> p a c").bitcast(I32))
-        w3_raw = {(1, a): load_weight(w3, 1, a, 2 + a) for a in range(GROUPS)}
+        w3_raw = {(1, a): load_weight(w3, 1, a, "w0%d" % a) for a in range(GROUPS)}
 
-        v_s = big.tile([P, S], U8, name="v_s", tag="grouped0", align_bytes=64)
+        v_s = slot([P, S], U8, "v_s", "woven0")
         nc.vector.tensor_copy(out=v_s[:], in_=tab_s[:].indirect(offs_t[:]))
         v_w = []
         for a in range(GROUPS):
-            t = big.tile([P, S], U32, name="v_w%d" % a, tag="big%d" % (6 + a), align_bytes=64)
-            nc.vector.tensor_copy(out=t[:], in_=tab_w[a][:].bitcast(U32).indirect(offs_t[:]))
-            v_w.append(t)
+            words = slot([P, S], U32, "v_w%d" % a, "v%d" % a)
+            nc.vector.tensor_copy(out=words[:], in_=tab_w[a][:].bitcast(U32).indirect(offs_t[:]))
+            v_w.append(words)
 
         neg_gh = keep.tile([P, GROUPS, PACK], F32, name="neg_gh")
         nc.gpsimd.tensor_scalar(out=neg_gh[:], in0=gh_t[:], scalar1=-1.0, scalar2=0.0, op0=ALU.mult, op1=ALU.add)
@@ -143,171 +166,155 @@ def tile_list_slab_bookmatch_features_kernel(
         def first_stage(g):
             for t in range(PACK):
                 h[g, t] = keep.tile([P, S], F32, name="h%d%d" % (g, t))
+                dealt = slice(t * P, (t + 1) * P)
                 for c0 in range(0, S, BANK):
-                    acc = psum.tile([P, BANK], F32, name="h_acc", tag="bank%d" % (2 * t + c0 // BANK))
+                    cols = slice(c0, c0 + BANK)
+                    acc = psum.tile([P, BANK], F32, name="h_acc", tag="bank%d" % ((t * S + c0) // BANK))
                     for a in (1, 0):
                         codes, scales = w1_q[g, a]
                         nc.tensor.matmul_mx(
-                            out=acc[:],
-                            lhsT=codes[:, t * P:(t + 1) * P].bitcast(FP8X4), lhsT_scale=scales[:, t * P:(t + 1) * P],
-                            rhs=v_w[a][:, c0:c0 + BANK].bitcast(FP8X4), rhs_scale=v_s[4 * a:P, c0:c0 + BANK],
+                            out=acc[:], lhsT=codes[:, dealt].bitcast(FP8X4), lhsT_scale=scales[:, dealt],
+                            rhs=v_w[a][:, cols].bitcast(FP8X4), rhs_scale=v_s[SCALE_ROWS * a:P, cols],
                             start=(a == 1), stop=(a == 0))
-                    nc.scalar.activation(out=h[g, t][:, c0:c0 + BANK], in_=acc[:], func=ACT.Identity,
-                                         bias=b1_t[:, g, t:t + 1])
+                    nc.scalar.activation(out=h[g, t][:, cols], in_=acc[:], func=ACT.Identity, bias=b1_t[:, g, t:t + 1])
 
-        d00 = round_weight(w1_raw[0, 0], "ss")
-        d01 = round_weight(w1_raw[0, 1], "sv", "dealt1")
-        w1_q[0, 0] = quantise(d00, "w1q00")
-        w1_q[0, 1] = quantise(d01, "w1q01")
+        w1_00 = round_weight(w1_raw[0, 0], rounded_slot("rounded0"), (on_scalar, on_scalar))
+        w1_01 = round_weight(w1_raw[0, 1], rounded_slot("rounded1"), (on_scalar, on_vector))
+        w1_q[0, 0] = quantise(w1_00, "w1_00")
+        w1_q[0, 1] = quantise(w1_01, "w1_01")
         first_stage(0)
-        d10 = round_weight(w1_raw[1, 0], "sv", "dealt2")
-        d11 = round_weight(w1_raw[1, 1], "vv", "dealt0")
-        w1_q[1, 0] = quantise(d10, "w1q10")
-        w1_q[1, 1] = quantise(d11, "w1q11")
+        w1_10 = round_weight(w1_raw[1, 0], rounded_slot("rounded2"), (on_vector, on_vector))
+        w1_11 = round_weight(w1_raw[1, 1], rounded_slot("rounded0"), (on_vector, on_vector))
+        w1_q[1, 0] = quantise(w1_10, "w1_10")
+        w1_q[1, 1] = quantise(w1_11, "w1_11")
         first_stage(1)
-        for a in range(GROUPS):
-            w3_raw[0, 1 - a] = load_weight(w3, 0, 1 - a, 6 + a)
+        w3_raw[0, 1] = load_weight(w3, 0, 1, "v0")
+        w3_raw[0, 0] = load_weight(w3, 0, 0, "v1")
 
         def pick(g, pos_t):
-            planes = big.tile([P, PACK, CUTS], BF16, name="planes", tag="planes%d" % g, align_bytes=64)
+            planes = slot([P, PACK, CUTS], BF16, "planes", "planes%d" % g)
             for t in range(PACK):
                 nc.vector.tensor_copy(out=planes[:, t, :], in_=h[g, t][:].indirect(pos_t[:]))
             return planes
 
-        def weave(planes, engines, tag):
-            grouped = big.tile([P, CUTS * PACK], BF16, name="grouped", tag=tag, align_bytes=64)
-            n = CUTS // len(engines)
-            for i, eng in enumerate(engines):
-                interleave(eng, grouped[:, i * n * PACK:(i + 1) * n * PACK], planes[:, :, i * n:(i + 1) * n])
-            return grouped
+        def weave(planes, copy, tag):
+            return interleave(slot([P, CUTS * PACK], BF16, "woven", tag), planes, (copy,))
 
         x1_q = {}
         x2_q = {}
         w3_q = {}
         bent = {}
-        ghh = {}
 
         def bend(g, tag):
-            together = big.tile([P, PACK, CUTS], F32, name="bent_rows", tag=tag, align_bytes=64)
-            bent[g] = big.tile([P, PACK, CUTS], F32, name="bent", tag="big%d" % (4 + g), align_bytes=64)
+            plain = slot([P, PACK, CUTS], F32, "plain", tag)
+            bent[g] = slot([P, PACK, CUTS], F32, "bent", "w1%d" % g)
             for c in (0, 2, 1, 3):
                 n0 = g * GROUP + c * P
                 acc = psum.tile([P, CUTS], F32, name="bent_acc", tag="bank%d" % (PACK * g + c))
                 for a in range(GROUPS):
                     codes, scales = x1_q[a]
                     nc.tensor.matmul_mx(
-                        out=acc[:],
-                        lhsT=w4_w[:, a, 2 * n0:2 * (n0 + P)].bitcast(FP4X4), lhsT_scale=w4_s[:, a, n0:n0 + P],
-                        rhs=codes[:].bitcast(FP8X4), rhs_scale=scales[:],
+                        out=acc[:], lhsT=w4_w[:, a, 2 * n0:2 * (n0 + P)].bitcast(FP4X4),
+                        lhsT_scale=w4_s[:, a, n0:n0 + P], rhs=codes[:].bitcast(FP8X4), rhs_scale=scales[:],
                         start=(a == 0), stop=(a == GROUPS - 1))
-                rows = together[:, c, :]
-                nc.scalar.activation(out=rows, in_=acc[:], func=ACT.Tanh, bias=b2_t[g][:, c:c + 1])
-                nc.sync.dma_start(out=bent[g][32 * c:32 * (c + 1), :, :], in_=rows)
+                nc.scalar.activation(out=plain[:, c, :], in_=acc[:], func=ACT.Tanh, bias=b2_t[g][:, c:c + 1])
+                nc.sync.dma_start(out=bent[g][quadrant(c, QUAD), :, :], in_=plain[:, c, :])
 
-        def scaled_h(g, c0, c1, slot):
-            out = late[:, slot * WIDE:slot * WIDE + PACK * (c1 - c0)].rearrange("p (t c) -> p t c", t=PACK)
-            for t in range(PACK):
-                nc.scalar.activation(out=out[:, t, :], in_=h[g, t][:, c0:c1], func=ACT.Copy, scale=neg_gh[:, g, t:t + 1])
-            return out
-
-        p10 = pick(0, pos1_t)
-        p11 = pick(1, pos1_t)
-        g10 = weave(p10, "s", "grouped0")
-        g11 = weave(p11, "s", "grouped1")
-        x1_q[0] = quantise(g10, "x1q0")
-        p20 = pick(0, pos2_t)
-        x1_q[1] = quantise(g11, "x1q1")
-        d31 = round_weight(w3_raw[0, 1], "ss", "dealt1")
-        d30 = round_weight(w3_raw[0, 0], "ss", "dealt2")
-        bend(0, "big7")
-        g20 = weave(p20, "s", "late0")
+        p1_0 = pick(0, pos1_t)
+        p1_1 = pick(1, pos1_t)
+        x1_0 = weave(p1_0, on_scalar, "woven0")
+        x1_1 = weave(p1_1, on_scalar, "woven1")
+        x1_q[0] = quantise(x1_0, "x1_0")
+        p2_0 = pick(0, pos2_t)
+        x1_q[1] = quantise(x1_1, "x1_1")
+        w3_01 = round_weight(w3_raw[0, 1], rounded_slot("rounded1"), (on_scalar, on_scalar))
+        w3_00 = round_weight(w3_raw[0, 0], rounded_slot("rounded2"), (on_scalar, on_scalar))
+        bend(0, "v1")
+        x2_0 = weave(p2_0, on_scalar, "bias0")
         bend(1, "planes0")
-        p21 = pick(1, pos2_t)
-        w3_q[0, 1] = quantise(d31, "w3q01")
-        w3_q[0, 0] = quantise(d30, "w3q00")
-        g21 = weave(p21, "v", "grouped0")
-        x2_q[1] = quantise(g21, "x2q1")
-        x2_q[0] = quantise(g20, "x2q0")
+        p2_1 = pick(1, pos2_t)
+        w3_q[0, 1] = quantise(w3_01, "w3_01")
+        w3_q[0, 0] = quantise(w3_00, "w3_00")
+        x2_1 = weave(p2_1, on_vector, "woven0")
+        x2_q[1] = quantise(x2_1, "x2_1")
+        x2_q[0] = quantise(x2_0, "x2_0")
 
         def second_stage(g):
-            cut = []
+            rows = []
             for t in range(PACK):
+                dealt = slice(t * P, (t + 1) * P)
                 acc = psum.tile([P, CUTS], F32, name="cut_acc", tag="bank%d" % (PACK * g + t))
                 for a in (1, 0):
                     w_codes, w_scales = w3_q[g, a]
                     codes, scales = x2_q[a]
                     nc.tensor.matmul_mx(
-                        out=acc[:],
-                        lhsT=w_codes[:, t * P:(t + 1) * P].bitcast(FP8X4), lhsT_scale=w_scales[:, t * P:(t + 1) * P],
-                        rhs=codes[:].bitcast(FP8X4), rhs_scale=scales[:],
-                        start=(a == 1), stop=(a == 0))
-                row = work.tile([P, CUTS], F32, name="cut", tag="cut", bufs=8)
+                        out=acc[:], lhsT=w_codes[:, dealt].bitcast(FP8X4), lhsT_scale=w_scales[:, dealt],
+                        rhs=codes[:].bitcast(FP8X4), rhs_scale=scales[:], start=(a == 1), stop=(a == 0))
+                row = work.tile([P, CUTS], F32, name="cut", tag="cut", bufs=GROUPS * PACK)
                 nc.vector.scalar_tensor_tensor(out=row[:], in0=bent[g][:, t, :], scalar=amp_t[:, g, t:t + 1],
                                                in1=acc[:], op0=ALU.mult, op1=ALU.add)
-                cut.append(row)
-            return cut
+                rows.append(row)
+            return rows
 
-        def spread(g, cut, c0, c1, slot):
-            n = c1 - c0
-            y = big.tile([P, PACK, n], F32, name="y", tag="big%d" % slot, align_bytes=64)
-            where = pos3_t[:, c0 // 16:c1 // 16]
+        steps = [(g, c0, c1) for g in range(GROUPS) for c0, c1 in SPANS]
+        y_scales = keep.tile([P, GROUPS, S], U8, name="y_scales", align_bytes=ALIGN)
+        scaled_ring = slot([P, RING * PACK * SPAN_MAX], F32, "scaled_ring", "bias1")
+        w3_pair = slot([P, GROUPS * PACK * GROUP], BF16, "w3_pair", "bias0")
+        w3_1 = [w3_pair[:, PACK * GROUP * a:PACK * GROUP * (a + 1)] for a in range(GROUPS)]
+        scaled = {}
+
+        def scale_h(step):
+            g, c0, c1 = steps[step]
+            first = (step % RING) * PACK * SPAN_MAX
+            scaled[step] = scaled_ring[:, first:first + PACK * (c1 - c0)].rearrange("p (t c) -> p t c", t=PACK)
             for t in range(PACK):
-                if (g, c1) == (GROUPS - 1, S):
-                    nc.vector.tensor_tensor(out=y[:, t, :], in0=cut[t][:].indirect(where), in1=ghh[g, c0][:, t, :], op=ALU.add)
-                else:
-                    nc.vector.tensor_copy(out=y[:, t, :], in_=cut[t][:].indirect(where))
-                    nc.gpsimd.tensor_tensor(out=y[:, t, :], in0=y[:, t, :], in1=ghh[g, c0][:, t, :], op=ALU.add)
-            rows = out_0[g * GROUP:(g + 1) * GROUP, c0:c1].rearrange("(p t) j -> p t j", t=PACK)
-            nc.sync.dma_start(out=rows, in_=y[:])
+                nc.scalar.activation(out=scaled[step][:, t, :], in_=h[g, t][:, c0:c1], func=ACT.Copy,
+                                     scale=neg_gh[:, g, t:t + 1])
+
+        def spread(step, rows):
+            g, c0, c1 = steps[step]
+            y = slot([P, PACK, c1 - c0], F32, "y", Y_TAGS[step % RING])
+            entries = pos3_t[:, c0 // PER_COLUMN:c1 // PER_COLUMN]
+            for t in range(PACK):
+                nc.vector.tensor_tensor(out=y[:, t, :], in0=rows[t][:].indirect(entries), in1=scaled[step][:, t, :],
+                                        op=ALU.add)
+            nc.sync.dma_start(out=out_0[g * GROUP:(g + 1) * GROUP, c0:c1].rearrange("(p t) j -> p t j", t=PACK),
+                              in_=y[:])
             return y
 
-        def round_y(y, eng, step):
-            n = y.shape[2]
-            grouped = work.tile([P, n * PACK], BF16, name="y_grouped", tag="y_grouped", bufs=3, align_bytes=64)
-            part = n // len(eng)
-            for i, e in enumerate(eng):
-                interleave(e, grouped[:, i * part * PACK:(i + 1) * part * PACK], y[:, :, i * part:(i + 1) * part])
-            return grouped
+        def round_y(y, copies):
+            woven = work.tile([P, y.shape[2] * PACK], BF16, name="y_woven", tag="y_woven", align_bytes=ALIGN)
+            return interleave(woven, y, copies)
 
-        def planes_out(g, grouped, y_s, c0, c1):
-            codes = work.tile([P, c1 - c0], U32, name="y_codes", tag="y_codes", align_bytes=64)
-            nc.vector.quantize_mx(out=codes[:].bitcast(FP8X4), scales=y_s[:, g, c0:c1], in_=grouped[:])
+        def store_codes(step, woven):
+            g, c0, c1 = steps[step]
+            codes = work.tile([P, c1 - c0], U32, name="y_codes", tag="y_codes", align_bytes=ALIGN)
+            nc.vector.quantize_mx(out=codes[:].bitcast(FP8X4), scales=y_scales[:, g, c0:c1], in_=woven[:])
             words = out_1[g].rearrange("p m t -> p (m t)").bitcast(I32)
             nc.sync.dma_start(out=words[:, c0:c1], in_=codes[:].bitcast(I32))
 
-        y_scales = keep.tile([P, GROUPS, S], U8, name="y_s", align_bytes=64)
-        steps = [(g, c0, c1) for g in range(GROUPS) for c0, c1 in SLICES]
-
-        def scale_step(step):
-            if FUSED and step < len(steps):
-                g, c0, c1 = steps[step]
-                ghh[g, c0] = scaled_h(g, c0, c1, step % 3)
-
-        late = big.tile([P, 3 * WIDE], F32, name="late", tag="late1", align_bytes=64) if FUSED else None
-        late_pair = big.tile([P, 2 * PACK * GROUP], BF16, name="late_pair", tag="late0", align_bytes=64)
-        late_bf16 = [late_pair[:, PACK * GROUP * a:PACK * GROUP * (a + 1)] for a in range(2)]
-        scale_step(0)
+        scale_h(0)
         cut = {0: second_stage(0)}
-        scale_step(1)
+        scale_h(1)
         for a in range(GROUPS):
-            round_weight(w3_raw[1, a], "ss", dealt=late_bf16[a])
-        scale_step(2)
-        pending = []
+            round_weight(w3_raw[1, a], w3_1[a], (on_scalar, on_scalar))
+        scale_h(2)
+        y_woven = {}
         for step, (g, c0, c1) in enumerate(steps):
-            if step == 3:
-                cut[1] = second_stage(1)
-            y = spread(g, cut[g], c0, c1, Y_SLOTS[step])
-            if step == 1:
-                both = big.tile([P, GROUPS * GROUP], U32, name="w3q1c", tag="big4", align_bytes=64)
+            if g not in cut:
+                cut[g] = second_stage(g)
+            y = spread(step, cut[g])
+            if step == len(SPANS) - 2:
+                both = slot([P, GROUPS * GROUP], U32, "w3_1_codes", "w10")
                 for a in range(GROUPS):
-                    w3_q[1, a] = quantise(late_bf16[a], "w3q1%d" % a, both[:, a * GROUP:(a + 1) * GROUP])
-            if len(pending) == LAG:
-                planes_out(*pending.pop(0))
-            last = (g, c1) == (GROUPS - 1, S)
-            pending.append((g, round_y(y, "v" if last else "s", step), y_scales, c0, c1))
-            scale_step(step + 3)
-        for item in pending:
-            planes_out(*item)
-        for q in range(4):
-            nc.scalar.dma_start(out=out_2[:, 4 * q:4 * q + 4, :].rearrange("g r c -> r g c").bitcast(I32),
-                                in_=y_scales[32 * q:32 * q + 4, :, :].bitcast(I32))
+                    w3_q[1, a] = quantise_into(both[:, a * GROUP:(a + 1) * GROUP], w3_1[a], "w3_1%d" % a)
+            if step >= LAG:
+                store_codes(step - LAG, y_woven[step - LAG])
+            y_woven[step] = round_y(y, (on_vector, on_scalar) if step == len(steps) - 1 else (on_scalar,))
+            if step + RING < len(steps):
+                scale_h(step + RING)
+        for step in range(len(steps) - LAG, len(steps)):
+            store_codes(step, y_woven[step])
+        for q in range(QUADRANTS):
+            nc.scalar.dma_start(out=out_2[:, scale_rows(q), :].rearrange("g r c -> r g c").bitcast(I32),
+                                in_=y_scales[quadrant(q, SCALE_ROWS), :, :].bitcast(I32))

from contextlib import ExitStack

import concourse.mybir as mybir

K, T, H, S, CUTS = 1024, 2048, 1024, 1024, 512
FLOPS = 2 * K * H * S + 2 * 2 * H * H * CUTS

F32 = mybir.dt.float32
BF16 = mybir.dt.bfloat16
I32 = mybir.dt.int32
U32 = mybir.dt.uint32
U16 = mybir.dt.uint16
U8 = mybir.dt.uint8
FP8X4 = mybir.dt.float8_e4m3fn_x4
FP4X4 = mybir.dt.float4_e2m1fn_x4
ACT = mybir.ActivationFunctionType
ALU = mybir.AluOpType

P = 128
PACK = 4
GROUP = P * PACK
GROUPS = 2
QUADRANTS = 4
QUAD = P // QUADRANTS
SCALE_ROWS = 4
BANK = 512
PER_COLUMN = 16
ALIGN = 64
RUN = 4
SPANS = ((0, 384), (384, 768), (768, 1024))
SPAN_MAX = 384
RING = 3
Y_TAGS = ("tab0", "tab1", "v0")
LAG = 2


def tile_list_slab_bookmatch_features_kernel(
    tc, tab_words, tab_scales, offs, pos1, pos2, pos3, w1, b1, w4_words, w4_scales, b2, amp, w3, gh,
    out_0, out_1, out_2,
):
    nc = tc.nc
    with ExitStack() as ctx:
        keep = ctx.enter_context(tc.tile_pool(name="keep", bufs=1))
        slots = ctx.enter_context(tc.tile_pool(name="slots", bufs=1))
        work = ctx.enter_context(tc.tile_pool(name="work", bufs=RING))
        psum = ctx.enter_context(tc.psum_pool(name="psum", bufs=1))

        def on_scalar(out, in_):
            nc.scalar.copy(out=out, in_=in_)

        def on_vector(out, in_):
            nc.vector.tensor_copy(out=out, in_=in_)

        def slot(shape, dtype, name, tag):
            return slots.tile(shape, dtype, name=name, tag=tag, align_bytes=ALIGN)

        def quadrant(q, rows):
            return slice(QUAD * q, QUAD * q + rows)

        def scale_rows(q):
            return slice(SCALE_ROWS * q, SCALE_ROWS * (q + 1))

        def load_list(src, name):
            tile = keep.tile(list(src.shape), U16, name=name)
            nc.sync.dma_start(out=tile[:], in_=src)
            return tile

        def load_dealt(vec, name):
            tile = keep.tile([P, GROUPS, PACK], F32, name=name)
            nc.sync.dma_start(out=tile[:], in_=vec.rearrange("(g p t) -> p g t", g=GROUPS, t=PACK))
            return tile

        def load_weight(w, g, a, tag, parts=1):
            raw = slot([P, PACK, GROUP], F32, "raw", tag)
            rows = w[a * GROUP:(a + 1) * GROUP, g * GROUP:(g + 1) * GROUP].rearrange("(p j) c -> p j c", j=PACK)
            width = GROUP // parts
            for i in range(parts):
                cols = slice(i * width, (i + 1) * width)
                nc.sync.dma_start(out=raw[:, :, cols], in_=rows[:, :, cols])
            return raw

        def load_table(a):
            tile = slot([P, T], I32, "tab_w", "tab%d" % a)
            nc.sync.dma_start(out=tile[:], in_=tab_words[a].rearrange("p t i -> p (t i)").bitcast(I32))
            return tile

        def round_weight(raw, rounded, copies):
            dst = rounded[:].rearrange("p (t m j) -> p m t j", t=PACK, j=PACK)
            src = raw[:].rearrange("p j (m t) -> p m t j", t=PACK)
            half = P // 2
            for i, copy in enumerate(copies):
                copy(dst[:, i * half:(i + 1) * half], src[:, i * half:(i + 1) * half])
            return rounded

        def rounded_slot(tag):
            return slot([P, GROUP * PACK], BF16, "rounded", tag)

        def quantise_into(codes, values, name):
            scales = keep.tile([P, GROUP], U8, name=name + "_scales", align_bytes=ALIGN)
            nc.vector.quantize_mx(out=codes[:].bitcast(FP8X4), scales=scales[:], in_=values[:])
            return codes, scales

        def quantise(values, name):
            return quantise_into(keep.tile([P, GROUP], U32, name=name + "_codes", align_bytes=ALIGN), values, name)

        def interleave(woven, planes, copies):
            share = planes.shape[2] // len(copies)
            for i, copy in enumerate(copies):
                dst = woven[:, i * share * PACK:(i + 1) * share * PACK]
                src = planes[:, :, i * share:(i + 1) * share]
                copy(dst.rearrange("p (c i t) -> p c t i", i=RUN, t=PACK), src.rearrange("p t (c i) -> p c t i", i=RUN))
            return woven

        tab_s = keep.tile([P, T], U8, name="tab_s")
        w4_s = keep.tile([P, GROUPS, H], U8, name="w4_s", align_bytes=ALIGN)
        nc.vector.memset(tab_s[:].bitcast(I32), 0)
        nc.gpsimd.memset(w4_s[:].bitcast(I32), 0)
        offs_t = load_list(offs, "offs_t")
        staged_s = keep.tile([P, T // 4], I32, name="staged_s")
        for q in range(QUADRANTS):
            nc.sync.dma_start(out=staged_s[quadrant(q, GROUPS * SCALE_ROWS), :],
                              in_=tab_scales[:, scale_rows(q), :].bitcast(I32))
        for q in range(QUADRANTS):
            live = quadrant(q, GROUPS * SCALE_ROWS)
            nc.vector.tensor_copy(out=tab_s[live, :].bitcast(I32), in_=staged_s[live, :])
        w1_raw = {}
        tab_w = [load_table(0)]
        w1_raw[0, 0] = load_weight(w1, 0, 0, "w00")
        tab_w.append(load_table(1))
        w1_raw[0, 1] = load_weight(w1, 0, 1, "w01", parts=2)
        b1_t = load_dealt(b1, "b1_t")
        w1_raw[1, 0] = load_weight(w1, 1, 0, "w10")
        w1_raw[1, 1] = load_weight(w1, 1, 1, "w11")
        pos1_t = load_list(pos1, "pos1_t")
        pos2_t = load_list(pos2, "pos2_t")
        pos3_t = load_list(pos3, "pos3_t")
        amp_t = load_dealt(amp, "amp_t")
        gh_t = load_dealt(gh, "gh_t")
        b2_t = []
        for g in range(GROUPS):
            bias = slot([P, PACK], F32, "b2_t", "bias%d" % g)
            with nc.allow_non_contiguous_dma(reason="one bias value for each partition"):
                nc.sync.dma_start(out=bias[:], in_=b2[g * GROUP:(g + 1) * GROUP].rearrange("(c p) -> p c", p=P))
            b2_t.append(bias)
        for q in range(QUADRANTS):
            nc.sync.dma_start(out=w4_s[quadrant(q, SCALE_ROWS), :, :].bitcast(I32),
                              in_=w4_scales[:, scale_rows(q), :].rearrange("a r c -> r a c").bitcast(I32))
        w4_w = keep.tile([P, GROUPS, 2 * H], U8, name="w4_w", align_bytes=ALIGN)
        nc.sync.dma_start(out=w4_w[:].bitcast(I32), in_=w4_words.rearrange("a p c -> p a c").bitcast(I32))
        w3_raw = {(1, a): load_weight(w3, 1, a, "w0%d" % a) for a in range(GROUPS)}

        v_s = slot([P, S], U8, "v_s", "woven0")
        nc.vector.tensor_copy(out=v_s[:], in_=tab_s[:].indirect(offs_t[:]))
        v_w = []
        for a in range(GROUPS):
            words = slot([P, S], U32, "v_w%d" % a, "v%d" % a)
            nc.vector.tensor_copy(out=words[:], in_=tab_w[a][:].bitcast(U32).indirect(offs_t[:]))
            v_w.append(words)

        neg_gh = keep.tile([P, GROUPS, PACK], F32, name="neg_gh")
        nc.gpsimd.tensor_scalar(out=neg_gh[:], in0=gh_t[:], scalar1=-1.0, scalar2=0.0, op0=ALU.mult, op1=ALU.add)

        w1_q = {}
        h = {}

        def first_stage(g):
            for t in range(PACK):
                h[g, t] = keep.tile([P, S], F32, name="h%d%d" % (g, t))
                dealt = slice(t * P, (t + 1) * P)
                for c0 in range(0, S, BANK):
                    cols = slice(c0, c0 + BANK)
                    acc = psum.tile([P, BANK], F32, name="h_acc", tag="bank%d" % ((t * S + c0) // BANK))
                    for a in (1, 0):
                        codes, scales = w1_q[g, a]
                        nc.tensor.matmul_mx(
                            out=acc[:], lhsT=codes[:, dealt].bitcast(FP8X4), lhsT_scale=scales[:, dealt],
                            rhs=v_w[a][:, cols].bitcast(FP8X4), rhs_scale=v_s[SCALE_ROWS * a:P, cols],
                            start=(a == 1), stop=(a == 0))
                    nc.scalar.activation(out=h[g, t][:, cols], in_=acc[:], func=ACT.Identity, bias=b1_t[:, g, t:t + 1])

        w1_00 = round_weight(w1_raw[0, 0], rounded_slot("rounded0"), (on_scalar, on_scalar))
        w1_01 = round_weight(w1_raw[0, 1], rounded_slot("rounded1"), (on_scalar, on_vector))
        w1_q[0, 0] = quantise(w1_00, "w1_00")
        w1_q[0, 1] = quantise(w1_01, "w1_01")
        first_stage(0)
        w1_10 = round_weight(w1_raw[1, 0], rounded_slot("rounded2"), (on_vector, on_vector))
        w1_11 = round_weight(w1_raw[1, 1], rounded_slot("rounded0"), (on_vector, on_vector))
        w1_q[1, 0] = quantise(w1_10, "w1_10")
        w1_q[1, 1] = quantise(w1_11, "w1_11")
        first_stage(1)
        w3_raw[0, 1] = load_weight(w3, 0, 1, "v0")
        w3_raw[0, 0] = load_weight(w3, 0, 0, "v1")

        def pick(g, pos_t):
            planes = slot([P, PACK, CUTS], BF16, "planes", "planes%d" % g)
            for t in range(PACK):
                nc.vector.tensor_copy(out=planes[:, t, :], in_=h[g, t][:].indirect(pos_t[:]))
            return planes

        def weave(planes, copy, tag):
            return interleave(slot([P, CUTS * PACK], BF16, "woven", tag), planes, (copy,))

        x1_q = {}
        x2_q = {}
        w3_q = {}
        bent = {}

        def bend(g, tag):
            plain = slot([P, PACK, CUTS], F32, "plain", tag)
            bent[g] = slot([P, PACK, CUTS], F32, "bent", "w1%d" % g)
            for c in (0, 2, 1, 3):
                n0 = g * GROUP + c * P
                acc = psum.tile([P, CUTS], F32, name="bent_acc", tag="bank%d" % (PACK * g + c))
                for a in range(GROUPS):
                    codes, scales = x1_q[a]
                    nc.tensor.matmul_mx(
                        out=acc[:], lhsT=w4_w[:, a, 2 * n0:2 * (n0 + P)].bitcast(FP4X4),
                        lhsT_scale=w4_s[:, a, n0:n0 + P], rhs=codes[:].bitcast(FP8X4), rhs_scale=scales[:],
                        start=(a == 0), stop=(a == GROUPS - 1))
                nc.scalar.activation(out=plain[:, c, :], in_=acc[:], func=ACT.Tanh, bias=b2_t[g][:, c:c + 1])
                nc.sync.dma_start(out=bent[g][quadrant(c, QUAD), :, :], in_=plain[:, c, :])

        p1_0 = pick(0, pos1_t)
        p1_1 = pick(1, pos1_t)
        x1_0 = weave(p1_0, on_scalar, "woven0")
        x1_1 = weave(p1_1, on_scalar, "woven1")
        x1_q[0] = quantise(x1_0, "x1_0")
        p2_0 = pick(0, pos2_t)
        x1_q[1] = quantise(x1_1, "x1_1")
        w3_01 = round_weight(w3_raw[0, 1], rounded_slot("rounded1"), (on_scalar, on_scalar))
        w3_00 = round_weight(w3_raw[0, 0], rounded_slot("rounded2"), (on_scalar, on_scalar))
        bend(0, "v1")
        x2_0 = weave(p2_0, on_scalar, "bias0")
        bend(1, "planes0")
        p2_1 = pick(1, pos2_t)
        w3_q[0, 1] = quantise(w3_01, "w3_01")
        w3_q[0, 0] = quantise(w3_00, "w3_00")
        x2_1 = weave(p2_1, on_vector, "woven0")
        x2_q[1] = quantise(x2_1, "x2_1")
        x2_q[0] = quantise(x2_0, "x2_0")

        def second_stage(g):
            rows = []
            for t in range(PACK):
                dealt = slice(t * P, (t + 1) * P)
                acc = psum.tile([P, CUTS], F32, name="cut_acc", tag="bank%d" % (PACK * g + t))
                for a in (1, 0):
                    w_codes, w_scales = w3_q[g, a]
                    codes, scales = x2_q[a]
                    nc.tensor.matmul_mx(
                        out=acc[:], lhsT=w_codes[:, dealt].bitcast(FP8X4), lhsT_scale=w_scales[:, dealt],
                        rhs=codes[:].bitcast(FP8X4), rhs_scale=scales[:], start=(a == 1), stop=(a == 0))
                row = work.tile([P, CUTS], F32, name="cut", tag="cut", bufs=GROUPS * PACK)
                nc.vector.scalar_tensor_tensor(out=row[:], in0=bent[g][:, t, :], scalar=amp_t[:, g, t:t + 1],
                                               in1=acc[:], op0=ALU.mult, op1=ALU.add)
                rows.append(row)
            return rows

        steps = [(g, c0, c1) for g in range(GROUPS) for c0, c1 in SPANS]
        y_scales = keep.tile([P, GROUPS, S], U8, name="y_scales", align_bytes=ALIGN)
        scaled_ring = slot([P, RING * PACK * SPAN_MAX], F32, "scaled_ring", "bias1")
        w3_pair = slot([P, GROUPS * PACK * GROUP], BF16, "w3_pair", "bias0")
        w3_1 = [w3_pair[:, PACK * GROUP * a:PACK * GROUP * (a + 1)] for a in range(GROUPS)]
        scaled = {}

        def scale_h(step):
            g, c0, c1 = steps[step]
            first = (step % RING) * PACK * SPAN_MAX
            scaled[step] = scaled_ring[:, first:first + PACK * (c1 - c0)].rearrange("p (t c) -> p t c", t=PACK)
            for t in range(PACK):
                nc.scalar.activation(out=scaled[step][:, t, :], in_=h[g, t][:, c0:c1], func=ACT.Copy,
                                     scale=neg_gh[:, g, t:t + 1])

        def spread(step, rows):
            g, c0, c1 = steps[step]
            y = slot([P, PACK, c1 - c0], F32, "y", Y_TAGS[step % RING])
            entries = pos3_t[:, c0 // PER_COLUMN:c1 // PER_COLUMN]
            for t in range(PACK):
                nc.vector.tensor_tensor(out=y[:, t, :], in0=rows[t][:].indirect(entries), in1=scaled[step][:, t, :],
                                        op=ALU.add)
            nc.sync.dma_start(out=out_0[g * GROUP:(g + 1) * GROUP, c0:c1].rearrange("(p t) j -> p t j", t=PACK),
                              in_=y[:])
            return y

        def round_y(y, copies):
            woven = work.tile([P, y.shape[2] * PACK], BF16, name="y_woven", tag="y_woven", align_bytes=ALIGN)
            return interleave(woven, y, copies)

        def store_codes(step, woven):
            g, c0, c1 = steps[step]
            codes = work.tile([P, c1 - c0], U32, name="y_codes", tag="y_codes", align_bytes=ALIGN)
            nc.vector.quantize_mx(out=codes[:].bitcast(FP8X4), scales=y_scales[:, g, c0:c1], in_=woven[:])
            words = out_1[g].rearrange("p m t -> p (m t)").bitcast(I32)
            nc.sync.dma_start(out=words[:, c0:c1], in_=codes[:].bitcast(I32))

        scale_h(0)
        cut = {0: second_stage(0)}
        scale_h(1)
        for a in range(GROUPS):
            round_weight(w3_raw[1, a], w3_1[a], (on_scalar, on_scalar))
        scale_h(2)
        y_woven = {}
        for step, (g, c0, c1) in enumerate(steps):
            if g not in cut:
                cut[g] = second_stage(g)
            y = spread(step, cut[g])
            if step == len(SPANS) - 2:
                both = slot([P, GROUPS * GROUP], U32, "w3_1_codes", "w10")
                for a in range(GROUPS):
                    w3_q[1, a] = quantise_into(both[:, a * GROUP:(a + 1) * GROUP], w3_1[a], "w3_1%d" % a)
            if step >= LAG:
                store_codes(step - LAG, y_woven[step - LAG])
            y_woven[step] = round_y(y, (on_vector, on_scalar) if step == len(steps) - 1 else (on_scalar,))
            if step + RING < len(steps):
                scale_h(step + RING)
        for step in range(len(steps) - LAG, len(steps)):
            store_codes(step, y_woven[step])
        for q in range(QUADRANTS):
            nc.scalar.dma_start(out=out_2[:, scale_rows(q), :].rearrange("g r c -> r g c").bitcast(I32),
                                in_=y_scales[quadrant(q, SCALE_ROWS), :, :].bitcast(I32))
